import numpy as np
import ml_dtypes

BF16 = ml_dtypes.bfloat16


def bf(x):
    return np.asarray(x, np.float32).astype(BF16)


def f32(x):
    return np.asarray(x, np.float32)


def f64(x):
    return np.asarray(x).astype(np.float64)


def striped(idx):
    return np.tile(idx.reshape(-1, 16).T, (8, 1))


def rows(idx, k):
    return np.tile(idx, (k, 1))


def look(tab, idx):
    return np.take_along_axis(f64(tab), rows(idx, len(tab)), axis=1)


K, S, V, N, M = 512, 2048, 1536, 1536, 512


def angles():
    a = np.random.uniform(0.0, 2.0 * np.pi, (K, S))
    return np.stack([np.cos(a), np.sin(a)])


def setup_inputs():
    return {"tab": bf(angles()), "x0": bf(np.random.standard_normal((K, V))), "x1": bf(np.random.standard_normal((K, V))), "w": bf(np.random.standard_normal((K, M)) / np.sqrt(K)), "b": f32(0.5 * np.random.standard_normal((M, 1))), "offs": striped(np.random.randint(0, S, N))}


def reference(tab, x0, x1, w, b, offs):
    idx = offs[:16].T.reshape(-1)
    x = f64(x0) * look(tab[0], idx) + f64(x1) * look(tab[1], idx)
    y = f64(w).T @ x
    return np.maximum(y + f64(b), 0.0)

@@ -1,0 +1,80 @@
+import concourse.mybir as mybir
+
+BF16, F32, U16 = mybir.dt.bfloat16, mybir.dt.float32, mybir.dt.uint16
+ALU = mybir.AluOpType
+RELU = mybir.ActivationFunctionType.Relu
+
+P = 128
+PIECE = 512
+GROUP = 16
+FLOPS = 2 * 512 * 512 * 1536 + 3 * 512 * 1536
+
+
+def tile_lookup_rope_mul_relu_kernel(tc, tab, x0, x1, w, b, offs, out):
+    nc = tc.nc
+    tables, rows, positions = tab.shape
+    entries = x0.shape[1]
+    row_blocks, out_blocks, pieces = rows // P, w.shape[1] // P, entries // PIECE
+    early = pieces - 1
+    values = (x0, x1)
+    terms = [(r, t) for r in range(row_blocks) for t in range(tables)]
+
+    with (
+        tc.tile_pool(name="held", bufs=1) as held,
+        tc.tile_pool(name="products", bufs=4) as products,
+        tc.tile_pool(name="results", bufs=out_blocks * pieces) as results,
+        tc.psum_pool(name="sums", bufs=early * out_blocks) as sums,
+    ):
+        offsets = held.tile(list(offs.shape), U16, name="offsets")
+        nc.sync.dma_start(offsets[:], offs)
+
+        window, x_early, weights = {}, {}, {}
+        for r, t in terms:
+            block = slice(r * P, (r + 1) * P)
+            window[r, t] = held.tile([P, positions], BF16, name="window_%d_%d" % (r, t))
+            nc.sync.dma_start(window[r, t][:], tab[t, block, :])
+            x_early[r, t] = held.tile([P, early * PIECE], BF16, name="x_early_%d_%d" % (r, t))
+            nc.sync.dma_start(x_early[r, t][:], values[t][block, : early * PIECE])
+            if t == 0:
+                weights[r] = held.tile([P, out_blocks * P], BF16, name="weights_%d" % r)
+                nc.sync.dma_start(weights[r][:], w[block, :])
+        bias = held.tile([P, out_blocks], F32, name="bias")
+        with nc.allow_non_contiguous_dma(reason="one bias value for each partition and output block"):
+            nc.sync.dma_start(bias[:], b.rearrange("(m p) o -> p (m o)", p=P))
+        x_late = []
+        for t in range(tables):
+            x_late.append(held.tile([P, row_blocks, PIECE], BF16, name="x_late_%d" % t))
+            nc.sync.dma_start(x_late[t][:], values[t][:, early * PIECE :].rearrange("(r p) n -> p r n", p=P))
+
+        def look_up_and_multiply(r, t, j, x_piece, banks):
+            piece_offsets = offsets[:, j * PIECE // GROUP : (j + 1) * PIECE // GROUP]
+            product = products.tile([P, PIECE], BF16, name="product")
+            nc.vector.tensor_tensor(product[:], window[r, t][:].indirect(piece_offsets), x_piece, ALU.mult)
+            for m in range(out_blocks):
+                nc.tensor.matmul(banks[m][:], weights[r][:, m * P : (m + 1) * P], product[:],
+                                 start=(r, t) == terms[0], stop=(r, t) == terms[-1])
+
+        def finish(j, banks, share_with_vector):
+            for m in range(out_blocks):
+                result = results.tile([P, PIECE], F32, name="result")
+                if share_with_vector and m % 2 == 1:
+                    nc.vector.tensor_scalar(result[:], banks[m][:], bias[:, m : m + 1], 0.0, ALU.add, ALU.max)
+                else:
+                    nc.scalar.activation(result[:], banks[m][:], RELU, bias=bias[:, m : m + 1])
+                nc.sync.dma_start(out[m * P : (m + 1) * P, j * PIECE : (j + 1) * PIECE], result[:])
+
+        def new_banks():
+            return [sums.tile([P, PIECE], F32, name="bank") for m in range(out_blocks)]
+
+        early_banks = [new_banks() for j in range(early)]
+        for r in range(row_blocks):
+            for j in range(early):
+                for t in range(tables):
+                    look_up_and_multiply(r, t, j, x_early[r, t][:, j * PIECE : (j + 1) * PIECE], early_banks[j])
+                if r == row_blocks - 1:
+                    finish(j, early_banks[j], False)
+
+        late_banks = new_banks()
+        for r, t in terms:
+            look_up_and_multiply(r, t, early, x_late[t][:, r, :], late_banks)
+        finish(early, late_banks, True)

@@ -7,6 +7,7 @@ RELU = mybir.ActivationFunctionType.Relu
 P = 128
 PIECE = 512
 GROUP = 16
+WARM_UP = 8
 FLOPS = 2 * 512 * 512 * 1536 + 3 * 512 * 1536
 
 
@@ -21,12 +22,15 @@ def tile_lookup_rope_mul_relu_kernel(tc, tab, x0, x1, w, b, offs, out):
 
     with (
         tc.tile_pool(name="held", bufs=1) as held,
-        tc.tile_pool(name="products", bufs=4) as products,
+        tc.tile_pool(name="products", bufs=6) as products,
         tc.tile_pool(name="results", bufs=out_blocks * pieces) as results,
         tc.psum_pool(name="sums", bufs=early * out_blocks) as sums,
     ):
         offsets = held.tile(list(offs.shape), U16, name="offsets")
         nc.sync.dma_start(offsets[:], offs)
+
+        zeros = held.tile([P, PIECE], BF16, name="zeros")
+        nc.vector.memset(zeros[:], 0.0)
 
         window, x_early, weights = {}, {}, {}
         for r, t in terms:
@@ -34,7 +38,9 @@ def tile_lookup_rope_mul_relu_kernel(tc, tab, x0, x1, w, b, offs, out):
             window[r, t] = held.tile([P, positions], BF16, name="window_%d_%d" % (r, t))
             nc.sync.dma_start(window[r, t][:], tab[t, block, :])
             x_early[r, t] = held.tile([P, early * PIECE], BF16, name="x_early_%d_%d" % (r, t))
-            nc.sync.dma_start(x_early[r, t][:], values[t][block, : early * PIECE])
+            step = PIECE if (r, t) == terms[0] else early * PIECE
+            for lo in range(0, early * PIECE, step):
+                nc.sync.dma_start(x_early[r, t][:, lo : lo + step], values[t][block, lo : lo + step])
             if t == 0:
                 weights[r] = held.tile([P, out_blocks * P], BF16, name="weights_%d" % r)
                 nc.sync.dma_start(weights[r][:], w[block, :])
@@ -67,12 +73,13 @@ def tile_lookup_rope_mul_relu_kernel(tc, tab, x0, x1, w, b, offs, out):
             return [sums.tile([P, PIECE], F32, name="bank") for m in range(out_blocks)]
 
         early_banks = [new_banks() for j in range(early)]
-        for r in range(row_blocks):
+        for i in range(WARM_UP):
+            nc.tensor.matmul(early_banks[-1][-1][:], zeros[:, :P], zeros[:], start=True, stop=True)
+        for r, t in terms:
             for j in range(early):
-                for t in range(tables):
-                    look_up_and_multiply(r, t, j, x_early[r, t][:, j * PIECE : (j + 1) * PIECE], early_banks[j])
-                if r == row_blocks - 1:
-                    finish(j, early_banks[j], False)
+                look_up_and_multiply(r, t, j, x_early[r, t][:, j * PIECE : (j + 1) * PIECE], early_banks[j])
+        for j in range(early):
+            finish(j, early_banks[j], False)
 
         late_banks = new_banks()
         for r, t in terms:

@@ -22,7 +22,7 @@ def tile_lookup_rope_mul_relu_kernel(tc, tab, x0, x1, w, b, offs, out):
 
     with (
         tc.tile_pool(name="held", bufs=1) as held,
-        tc.tile_pool(name="products", bufs=6) as products,
+        tc.tile_pool(name="products", bufs=len(terms) * pieces) as products,
         tc.tile_pool(name="results", bufs=out_blocks * pieces) as results,
         tc.psum_pool(name="sums", bufs=early * out_blocks) as sums,
     ):
@@ -38,7 +38,7 @@ def tile_lookup_rope_mul_relu_kernel(tc, tab, x0, x1, w, b, offs, out):
             window[r, t] = held.tile([P, positions], BF16, name="window_%d_%d" % (r, t))
             nc.sync.dma_start(window[r, t][:], tab[t, block, :])
             x_early[r, t] = held.tile([P, early * PIECE], BF16, name="x_early_%d_%d" % (r, t))
-            step = PIECE if (r, t) == terms[0] else early * PIECE
+            step = PIECE if r == 0 else early * PIECE
             for lo in range(0, early * PIECE, step):
                 nc.sync.dma_start(x_early[r, t][:, lo : lo + step], values[t][block, lo : lo + step])
             if t == 0:
@@ -60,14 +60,19 @@ def tile_lookup_rope_mul_relu_kernel(tc, tab, x0, x1, w, b, offs, out):
                 nc.tensor.matmul(banks[m][:], weights[r][:, m * P : (m + 1) * P], product[:],
                                  start=(r, t) == terms[0], stop=(r, t) == terms[-1])
 
-        def finish(j, banks, share_with_vector):
+        def finish(j, banks, last):
             for m in range(out_blocks):
                 result = results.tile([P, PIECE], F32, name="result")
-                if share_with_vector and m % 2 == 1:
-                    nc.vector.tensor_scalar(result[:], banks[m][:], bias[:, m : m + 1], 0.0, ALU.add, ALU.max)
-                else:
-                    nc.scalar.activation(result[:], banks[m][:], RELU, bias=bias[:, m : m + 1])
-                nc.sync.dma_start(out[m * P : (m + 1) * P, j * PIECE : (j + 1) * PIECE], result[:])
+                step = PIECE // 2 if last and m == 0 else PIECE
+                for lo in range(0, PIECE, step):
+                    cols = slice(lo, lo + step)
+                    if last and m % 2 == 1:
+                        nc.vector.tensor_scalar(result[:, cols], banks[m][:, cols], bias[:, m : m + 1], 0.0,
+                                                ALU.add, ALU.max)
+                    else:
+                        nc.scalar.activation(result[:, cols], banks[m][:, cols], RELU, bias=bias[:, m : m + 1])
+                    nc.sync.dma_start(out[m * P : (m + 1) * P, j * PIECE + lo : j * PIECE + lo + step],
+                                      result[:, cols])
 
         def new_banks():
             return [sums.tile([P, PIECE], F32, name="bank") for m in range(out_blocks)]
@@ -75,10 +80,12 @@ def tile_lookup_rope_mul_relu_kernel(tc, tab, x0, x1, w, b, offs, out):
         early_banks = [new_banks() for j in range(early)]
         for i in range(WARM_UP):
             nc.tensor.matmul(early_banks[-1][-1][:], zeros[:, :P], zeros[:], start=True, stop=True)
-        for r, t in terms:
+        for r, t in terms[:-tables]:
             for j in range(early):
                 look_up_and_multiply(r, t, j, x_early[r, t][:, j * PIECE : (j + 1) * PIECE], early_banks[j])
         for j in range(early):
+            for r, t in terms[-tables:]:
+                look_up_and_multiply(r, t, j, x_early[r, t][:, j * PIECE : (j + 1) * PIECE], early_banks[j])
             finish(j, early_banks[j], False)
 
         late_banks = new_banks()

@@ -7,7 +7,6 @@ RELU = mybir.ActivationFunctionType.Relu
 P = 128
 PIECE = 512
 GROUP = 16
-WARM_UP = 8
 FLOPS = 2 * 512 * 512 * 1536 + 3 * 512 * 1536
 
 
@@ -28,9 +27,6 @@ def tile_lookup_rope_mul_relu_kernel(tc, tab, x0, x1, w, b, offs, out):
     ):
         offsets = held.tile(list(offs.shape), U16, name="offsets")
         nc.sync.dma_start(offsets[:], offs)
-
-        zeros = held.tile([P, PIECE], BF16, name="zeros")
-        nc.vector.memset(zeros[:], 0.0)
 
         window, x_early, weights = {}, {}, {}
         for r, t in terms:
@@ -78,8 +74,6 @@ def tile_lookup_rope_mul_relu_kernel(tc, tab, x0, x1, w, b, offs, out):
             return [sums.tile([P, PIECE], F32, name="bank") for m in range(out_blocks)]
 
         early_banks = [new_banks() for j in range(early)]
-        for i in range(WARM_UP):
-            nc.tensor.matmul(early_banks[-1][-1][:], zeros[:, :P], zeros[:], start=True, stop=True)
         for r, t in terms[:-tables]:
             for j in range(early):
                 look_up_and_multiply(r, t, j, x_early[r, t][:, j * PIECE : (j + 1) * PIECE], early_banks[j])

import concourse.mybir as mybir

BF16, F32, U16 = mybir.dt.bfloat16, mybir.dt.float32, mybir.dt.uint16
ALU = mybir.AluOpType
RELU = mybir.ActivationFunctionType.Relu

P = 128
PIECE = 512
GROUP = 16
FLOPS = 2 * 512 * 512 * 1536 + 3 * 512 * 1536


def tile_lookup_rope_mul_relu_kernel(tc, tab, x0, x1, w, b, offs, out):
    nc = tc.nc
    tables, rows, positions = tab.shape
    entries = x0.shape[1]
    row_blocks, out_blocks, pieces = rows // P, w.shape[1] // P, entries // PIECE
    early = pieces - 1
    values = (x0, x1)
    terms = [(r, t) for r in range(row_blocks) for t in range(tables)]

    with (
        tc.tile_pool(name="held", bufs=1) as held,
        tc.tile_pool(name="products", bufs=len(terms) * pieces) as products,
        tc.tile_pool(name="results", bufs=out_blocks * pieces) as results,
        tc.psum_pool(name="sums", bufs=early * out_blocks) as sums,
    ):
        offsets = held.tile(list(offs.shape), U16, name="offsets")
        nc.sync.dma_start(offsets[:], offs)

        window, x_early, weights = {}, {}, {}
        for r, t in terms:
            block = slice(r * P, (r + 1) * P)
            window[r, t] = held.tile([P, positions], BF16, name="window_%d_%d" % (r, t))
            nc.sync.dma_start(window[r, t][:], tab[t, block, :])
            x_early[r, t] = held.tile([P, early * PIECE], BF16, name="x_early_%d_%d" % (r, t))
            step = PIECE if r == 0 else early * PIECE
            for lo in range(0, early * PIECE, step):
                nc.sync.dma_start(x_early[r, t][:, lo : lo + step], values[t][block, lo : lo + step])
            if t == 0:
                weights[r] = held.tile([P, out_blocks * P], BF16, name="weights_%d" % r)
                nc.sync.dma_start(weights[r][:], w[block, :])
        bias = held.tile([P, out_blocks], F32, name="bias")
        with nc.allow_non_contiguous_dma(reason="one bias value for each partition and output block"):
            nc.sync.dma_start(bias[:], b.rearrange("(m p) o -> p (m o)", p=P))
        x_late = []
        for t in range(tables):
            x_late.append(held.tile([P, row_blocks, PIECE], BF16, name="x_late_%d" % t))
            nc.sync.dma_start(x_late[t][:], values[t][:, early * PIECE :].rearrange("(r p) n -> p r n", p=P))

        def look_up_and_multiply(r, t, j, x_piece, banks):
            piece_offsets = offsets[:, j * PIECE // GROUP : (j + 1) * PIECE // GROUP]
            product = products.tile([P, PIECE], BF16, name="product")
            nc.vector.tensor_tensor(product[:], window[r, t][:].indirect(piece_offsets), x_piece, ALU.mult)
            for m in range(out_blocks):
                nc.tensor.matmul(banks[m][:], weights[r][:, m * P : (m + 1) * P], product[:],
                                 start=(r, t) == terms[0], stop=(r, t) == terms[-1])

        def finish(j, banks, last):
            for m in range(out_blocks):
                result = results.tile([P, PIECE], F32, name="result")
                step = PIECE // 2 if last and m == 0 else PIECE
                for lo in range(0, PIECE, step):
                    cols = slice(lo, lo + step)
                    if last and m % 2 == 1:
                        nc.vector.tensor_scalar(result[:, cols], banks[m][:, cols], bias[:, m : m + 1], 0.0,
                                                ALU.add, ALU.max)
                    else:
                        nc.scalar.activation(result[:, cols], banks[m][:, cols], RELU, bias=bias[:, m : m + 1])
                    nc.sync.dma_start(out[m * P : (m + 1) * P, j * PIECE + lo : j * PIECE + lo + step],
                                      result[:, cols])

        def new_banks():
            return [sums.tile([P, PIECE], F32, name="bank") for m in range(out_blocks)]

        early_banks = [new_banks() for j in range(early)]
        for r, t in terms[:-tables]:
            for j in range(early):
                look_up_and_multiply(r, t, j, x_early[r, t][:, j * PIECE : (j + 1) * PIECE], early_banks[j])
        for j in range(early):
            for r, t in terms[-tables:]:
                look_up_and_multiply(r, t, j, x_early[r, t][:, j * PIECE : (j + 1) * PIECE], early_banks[j])
            finish(j, early_banks[j], False)

        late_banks = new_banks()
        for r, t in terms:
            look_up_and_multiply(r, t, early, x_late[t][:, r, :], late_banks)
        finish(early, late_banks, True)
